import numpy as np
import ml_dtypes


def mxq(x, axis, fmt="e4m3"):
    dtype, down = {"e4m3": (ml_dtypes.float8_e4m3fn, 7), "e5m2": (ml_dtypes.float8_e5m2, 14)}[fmt]
    v = np.moveaxis(np.asarray(x, np.float32).astype(ml_dtypes.bfloat16).astype(np.float64), axis, -1)
    blocks = v.reshape(v.shape[:-1] + (-1, 32))
    amax = np.abs(blocks).max(-1, keepdims=True)
    byte = np.maximum(np.where(amax > 0, np.frexp(amax)[1] - 1 + 127, 0) - down, 1)
    scale = np.exp2(byte - 127.0)
    codes = (blocks / scale).astype(np.float32).astype(dtype).astype(np.float64)
    return np.moveaxis((codes * scale).reshape(v.shape), -1, axis)


WIDE = False


def mx_kscale(k):
    if not WIDE:
        return np.ones(k)
    levels = np.array([10, -10, 5, -5, 0])
    if k % 512:
        return np.exp2(np.random.permutation(np.resize(levels, k // 32))).repeat(32)
    a = np.empty((k // 512, 16))
    for p in range(k // 512):
        a[p, :8] = np.random.permutation(np.resize(levels, 8))
        for g in range(8):
            far = levels[np.abs(levels - a[p, g]) >= 10]
            a[p, g + 8] = far[np.random.randint(len(far))]
    return np.exp2(a.ravel()).repeat(32)


def f64(x):
    return np.asarray(x).astype(np.float64)


def striped(idx):
    return np.tile(np.asarray(idx).reshape(-1, 16).T, (8, 1)).astype(np.uint16)


def unstriped(offs):
    return offs[:16].T.reshape(-1).astype(np.int64)


D, T, I, G, U, Q = 512, 2048, 1024, 128, 512, 256


def setup_inputs():
    n = np.random.standard_normal
    idx = np.random.permutation(T)[:I]
    idx2 = np.random.permutation(U)[:G]
    fd = mx_kscale(D)
    return {
        "query": (n((D, Q)) * 0.5 / np.sqrt(D) * fd[:, None]).astype(np.float32),
        "keys": (n((D, T))).astype(np.float32),
        "sg": (np.random.uniform(-1.0, 1.0, (1, I))).astype(np.float32),
        "dsc": (np.random.uniform(0.5, 1.5, (D, 1)) / fd[:, None]).astype(np.float32),
        "bias": (0.5 * n((Q, U))).astype(np.float32),
        "offs": striped(idx),
        "offs2": striped(idx2),
    }


def reference(query, keys, sg, dsc, bias, offs, offs2):
    idx = unstriped(offs)
    idx2 = unstriped(offs2)
    sk = (f64(keys)[:, idx] * f64(sg)).reshape(D, G, I // G).sum(axis=2) * f64(dsc)
    queryq = mxq(f64(query), 0, "e4m3")
    skq = mxq(sk, 0, "e4m3")
    a = queryq.T @ skq
    s = a + f64(bias)[:, idx2]
    p = np.exp(s - np.max(s, axis=1, keepdims=True))
    y = p / np.sum(p, axis=1, keepdims=True) * 128.0
    return y

@@ -1,0 +1,175 @@
+from contextlib import ExitStack
+
+import concourse.mybir as mybir
+from concourse.masks import make_identity
+
+D, T, I, G, U, Q = 512, 2048, 1024, 128, 512, 256
+FLOPS = 2 * D * Q * G
+
+F32 = mybir.dt.float32
+BF16 = mybir.dt.bfloat16
+U32 = mybir.dt.uint32
+U16 = mybir.dt.uint16
+U8 = mybir.dt.uint8
+FP8X4 = mybir.dt.float8_e4m3fn_x4
+ALU = mybir.AluOpType
+ACT = mybir.ActivationFunctionType
+AXIS = mybir.AxisListType
+
+P = 128
+PACK = 4
+PAGE = I // G
+HALF = I // 2
+ORDER = (2, 0, 1, 3)
+
+
+def tile_attend_pagesketch_kernel(tc, query, keys, sg, dsc, bias, offs, offs2, out):
+    nc = tc.nc
+    with ExitStack() as ctx:
+        lists = ctx.enter_context(tc.tile_pool(name="lists", bufs=1))
+        keep = ctx.enter_context(tc.tile_pool(name="keep", bufs=1))
+        once = ctx.enter_context(tc.psum_pool(name="once", bufs=1))
+        ring = ctx.enter_context(tc.psum_pool(name="ring", bufs=2))
+
+        slot_list = lists.tile([P, I // 16], U16, name="slot_list")
+        page_list = lists.tile([P, G // 16], U16, name="page_list")
+
+        sg_cols = keep.tile([P, 2, 4], F32, name="sg_cols")
+        dsc_cols = keep.tile([P, PACK], F32, name="dsc_cols")
+        with nc.allow_non_contiguous_dma(reason="short rows of two small vectors"):
+            nc.sync.dma_start(out=sg_cols[:], in_=sg.rearrange("o (h k j) -> k (o h) j", h=2, j=4))
+            nc.scalar.dma_start(out=dsc_cols[:], in_=dsc.rearrange("(p t) o -> p (t o)", t=PACK))
+
+        key_rows = keys.rearrange("(p t) n -> t p n", t=PACK)
+        planes = {}
+        for n, t in enumerate(ORDER):
+            planes[t] = keep.tile([P, T], F32, name="keys%d" % t)
+            nc.sync.dma_start(out=planes[t][:], in_=key_rows[t])
+            if n == 0:
+                nc.sync.dma_start(slot_list[:], offs)
+        q_raw = keep.tile([P, PACK, Q], F32, name="q_raw")
+        nc.sync.dma_start(out=q_raw[:], in_=query.rearrange("(p t) q -> p t q", t=PACK))
+        nc.sync.dma_start(page_list[:], offs2)
+        bias_rows = keep.tile([P, 2 * U], F32, name="bias_rows")
+        nc.sync.dma_start(
+            out=bias_rows[:].rearrange("p (h u) -> p h u", h=2),
+            in_=bias.rearrange("(h p) u -> p h u", h=2),
+        )
+
+        ident = keep.tile([P, P], F32, name="ident")
+        make_identity(nc, ident[:])
+
+        sg_row = keep.tile([P, I], F32, name="sg_row")
+        sg_dsc = keep.tile([P, I], F32, name="sg_dsc")
+        last = ORDER[-1]
+        spread = []
+        for h in range(2):
+            bank = once.tile([P, 4, P], F32, name="spread%d" % h)
+            for j in range(4):
+                nc.tensor.transpose(bank[:, j, :], sg_cols[:, h, j : j + 1].to_broadcast([P, P]), ident[:])
+            spread.append(bank)
+            src = bank[:].rearrange("p j k -> p k j")
+            dst = sg_row[:, h * HALF : (h + 1) * HALF].rearrange("p (k j) -> p k j", j=4)
+            if h == 0:
+                nc.vector.tensor_copy(out=dst, in_=src)
+            else:
+                nc.scalar.copy(out=dst, in_=src)
+        for h in range(2):
+            nc.scalar.activation(
+                out=sg_dsc[:, h * HALF : (h + 1) * HALF].rearrange("p (k j) -> p k j", j=4),
+                in_=spread[h][:].rearrange("p j k -> p k j"),
+                func=ACT.Copy,
+                scale=dsc_cols[:, last : last + 1],
+            )
+
+        sk = keep.tile([P, G, PACK], BF16, name="sk", align_bytes=64)
+        for n, t in enumerate(ORDER):
+            prod = keep.tile([P, I], F32, name="prod%d" % t)
+            factor = sg_dsc if t == last else sg_row
+            if n in (0, len(ORDER) - 1):
+                for h in range(2):
+                    cols = slice(h * HALF, (h + 1) * HALF)
+                    nc.vector.tensor_tensor(
+                        prod[:, cols],
+                        planes[t][:].indirect(slot_list[:, h * HALF // 16 : (h + 1) * HALF // 16]),
+                        factor[:, cols],
+                        ALU.mult,
+                    )
+            else:
+                nc.vector.tensor_tensor(prod[:], planes[t][:].indirect(slot_list[:]), factor[:], ALU.mult)
+            if t == last:
+                for h in range(2):
+                    with nc.allow_low_precision(reason="float32 sum, rounded once for the quantiser"):
+                        nc.vector.tensor_reduce(
+                            out=sk[:, h * G // 2 : (h + 1) * G // 2, t],
+                            in_=prod[:, h * HALF : (h + 1) * HALF].rearrange("p (g j) -> p g j", j=PAGE),
+                            axis=AXIS.X,
+                            op=ALU.add,
+                        )
+            else:
+                summed = ring.tile([P, P], F32, name="summed")
+                for j in range(PAGE):
+                    nc.tensor.matmul(
+                        summed[:], prod[:, j:I:PAGE], ident[:],
+                        start=(j == 0), stop=(j == PAGE - 1), is_transpose=True,
+                    )
+                turned = keep.tile([P, P], F32, name="turned%d" % t)
+                nc.scalar.copy(out=turned[:], in_=summed[:])
+                back = ring.tile([P, P], F32, name="back")
+                nc.tensor.transpose(back[:], turned[:], ident[:])
+                if t == last - 1:
+                    nc.scalar.activation(
+                        out=sk[:, :, t : t + 2],
+                        in_=back[:].unsqueeze(2).to_broadcast([P, G, 2]),
+                        func=ACT.Copy,
+                        scale=dsc_cols[:, t : t + 1],
+                    )
+                else:
+                    nc.scalar.activation(out=sk[:, :, t], in_=back[:], func=ACT.Copy, scale=dsc_cols[:, t : t + 1])
+
+        q_bf = keep.tile([P, Q, PACK], BF16, name="q_bf", align_bytes=64)
+        nc.scalar.copy(
+            out=q_bf[:].rearrange("p (c i) t -> p c t i", i=4),
+            in_=q_raw[:].rearrange("p t (c i) -> p c t i", i=4),
+        )
+        q_codes = keep.tile([P, Q], U32, name="q_codes", align_bytes=64)
+        q_scales = keep.tile([P, Q], U8, name="q_scales", align_bytes=64)
+        nc.vector.quantize_mx(
+            out=q_codes[:].bitcast(FP8X4), scales=q_scales[:], in_=q_bf[:].rearrange("p q t -> p (q t)")
+        )
+        sk_codes = keep.tile([P, G], U32, name="sk_codes", align_bytes=64)
+        sk_scales = keep.tile([P, G], U8, name="sk_scales", align_bytes=64)
+        nc.vector.quantize_mx(
+            out=sk_codes[:].bitcast(FP8X4), scales=sk_scales[:], in_=sk[:].rearrange("p g t -> p (g t)")
+        )
+
+        picked, scores, s, neg_max = [], [], [], []
+        for h in range(2):
+            picked.append(keep.tile([P, G], F32, name="picked%d" % h))
+            nc.vector.tensor_copy(picked[h][:], bias_rows[:, h * U : (h + 1) * U].indirect(page_list[:]))
+            scores.append(once.tile([P, G], F32, name="scores%d" % h))
+            rows = slice(h * P, (h + 1) * P)
+            nc.tensor.matmul_mx(
+                out=scores[h][:],
+                lhsT=q_codes[:, rows].bitcast(FP8X4),
+                lhsT_scale=q_scales[:, rows],
+                rhs=sk_codes[:].bitcast(FP8X4),
+                rhs_scale=sk_scales[:],
+                start=True,
+                stop=True,
+            )
+        for h in range(2):
+            s.append(keep.tile([P, G], F32, name="s%d" % h))
+            nc.vector.tensor_tensor(s[h][:], scores[h][:], picked[h][:], ALU.add)
+        for h in range(2):
+            neg_max.append(keep.tile([P, 1], F32, name="neg_max%d" % h))
+            nc.vector.tensor_reduce(out=neg_max[h][:], in_=s[h][:], axis=AXIS.X, op=ALU.max, negate=True)
+        for h in range(2):
+            p = keep.tile([P, G], F32, name="p%d" % h)
+            total = keep.tile([P, 1], F32, name="total%d" % h)
+            nc.scalar.activation(out=p[:], in_=s[h][:], func=ACT.Exp, bias=neg_max[h][:], accum_out=total[:])
+            inverse = keep.tile([P, 1], F32, name="inverse%d" % h)
+            nc.vector.reciprocal(inverse[:], total[:])
+            y = keep.tile([P, G], F32, name="y%d" % h)
+            nc.vector.tensor_scalar(y[:], p[:], inverse[:], float(G), ALU.mult, ALU.mult)
+            nc.sync.dma_start(out=out[h * P : (h + 1) * P, :], in_=y[:])

@@ -29,7 +29,6 @@ def tile_attend_pagesketch_kernel(tc, query, keys, sg, dsc, bias, offs, offs2, o
         lists = ctx.enter_context(tc.tile_pool(name="lists", bufs=1))
         keep = ctx.enter_context(tc.tile_pool(name="keep", bufs=1))
         once = ctx.enter_context(tc.psum_pool(name="once", bufs=1))
-        ring = ctx.enter_context(tc.psum_pool(name="ring", bufs=2))
 
         slot_list = lists.tile([P, I // 16], U16, name="slot_list")
         page_list = lists.tile([P, G // 16], U16, name="page_list")
@@ -60,79 +59,87 @@ def tile_attend_pagesketch_kernel(tc, query, keys, sg, dsc, bias, offs, offs2, o
         make_identity(nc, ident[:])
 
         sg_row = keep.tile([P, I], F32, name="sg_row")
-        sg_dsc = keep.tile([P, I], F32, name="sg_dsc")
-        last = ORDER[-1]
-        spread = []
         for h in range(2):
-            bank = once.tile([P, 4, P], F32, name="spread%d" % h)
+            spread = once.tile([P, 4, P], F32, name="spread%d" % h)
             for j in range(4):
-                nc.tensor.transpose(bank[:, j, :], sg_cols[:, h, j : j + 1].to_broadcast([P, P]), ident[:])
-            spread.append(bank)
-            src = bank[:].rearrange("p j k -> p k j")
+                nc.tensor.transpose(spread[:, j, :], sg_cols[:, h, j : j + 1].to_broadcast([P, P]), ident[:])
+            src = spread[:].rearrange("p j k -> p k j")
             dst = sg_row[:, h * HALF : (h + 1) * HALF].rearrange("p (k j) -> p k j", j=4)
             if h == 0:
                 nc.vector.tensor_copy(out=dst, in_=src)
             else:
                 nc.scalar.copy(out=dst, in_=src)
-        for h in range(2):
-            nc.scalar.activation(
-                out=sg_dsc[:, h * HALF : (h + 1) * HALF].rearrange("p (k j) -> p k j", j=4),
-                in_=spread[h][:].rearrange("p j k -> p k j"),
-                func=ACT.Copy,
-                scale=dsc_cols[:, last : last + 1],
+        first, second, third, last = ORDER
+        factor = {first: sg_row}
+        for t in ORDER[1:]:
+            factor[t] = keep.tile([P, I], F32, name="sg_dsc%d" % t)
+            nc.scalar.activation(out=factor[t][:], in_=sg_row[:], func=ACT.Copy, scale=dsc_cols[:, t : t + 1])
+
+        def gather(dst, t, lo, hi):
+            nc.vector.tensor_tensor(
+                dst, planes[t][:].indirect(slot_list[:, lo // 16 : hi // 16]), factor[t][:, lo:hi], ALU.mult
             )
 
-        sk = keep.tile([P, G, PACK], BF16, name="sk", align_bytes=64)
-        for n, t in enumerate(ORDER):
-            prod = keep.tile([P, I], F32, name="prod%d" % t)
-            factor = sg_dsc if t == last else sg_row
-            if n in (0, len(ORDER) - 1):
-                for h in range(2):
-                    cols = slice(h * HALF, (h + 1) * HALF)
-                    nc.vector.tensor_tensor(
-                        prod[:, cols],
-                        planes[t][:].indirect(slot_list[:, h * HALF // 16 : (h + 1) * HALF // 16]),
-                        factor[:, cols],
-                        ALU.mult,
-                    )
-            else:
-                nc.vector.tensor_tensor(prod[:], planes[t][:].indirect(slot_list[:]), factor[:], ALU.mult)
-            if t == last:
-                for h in range(2):
-                    with nc.allow_low_precision(reason="float32 sum, rounded once for the quantiser"):
-                        nc.vector.tensor_reduce(
-                            out=sk[:, h * G // 2 : (h + 1) * G // 2, t],
-                            in_=prod[:, h * HALF : (h + 1) * HALF].rearrange("p (g j) -> p g j", j=PAGE),
-                            axis=AXIS.X,
-                            op=ALU.add,
-                        )
-            else:
-                summed = ring.tile([P, P], F32, name="summed")
-                for j in range(PAGE):
-                    nc.tensor.matmul(
-                        summed[:], prod[:, j:I:PAGE], ident[:],
-                        start=(j == 0), stop=(j == PAGE - 1), is_transpose=True,
-                    )
-                turned = keep.tile([P, P], F32, name="turned%d" % t)
-                nc.scalar.copy(out=turned[:], in_=summed[:])
-                back = ring.tile([P, P], F32, name="back")
-                nc.tensor.transpose(back[:], turned[:], ident[:])
-                if t == last - 1:
-                    nc.scalar.activation(
-                        out=sk[:, :, t : t + 2],
-                        in_=back[:].unsqueeze(2).to_broadcast([P, G, 2]),
-                        func=ACT.Copy,
-                        scale=dsc_cols[:, t : t + 1],
-                    )
-                else:
-                    nc.scalar.activation(out=sk[:, :, t], in_=back[:], func=ACT.Copy, scale=dsc_cols[:, t : t + 1])
+        def page_sums(dst, prod):
+            for j in range(PAGE):
+                nc.tensor.matmul(
+                    dst, prod[:, j:I:PAGE], ident[:], start=(j == 0), stop=(j == PAGE - 1), is_transpose=True
+                )
 
-        q_bf = keep.tile([P, Q, PACK], BF16, name="q_bf", align_bytes=64)
+        sk = keep.tile([P, G, PACK], BF16, name="sk", align_bytes=64)
+        prod = {t: keep.tile([P, I], F32, name="prod%d" % t) for t in ORDER[:3]}
+        bank = {t: once.tile([P, 3, P], F32, name="bank%d" % t) for t in ORDER[:3]}
+        turned = {
+            first: keep.tile([P, P], F32, name="turned_first", tag="chain", align_bytes=64),
+            second: keep.tile([P, P], F32, name="turned_second"),
+            third: keep.tile([P, P], F32, name="turned_third"),
+        }
+
+        gather(prod[first][:, :HALF], first, 0, HALF)
+        gather(prod[first][:, HALF:], first, HALF, I)
+        page_sums(bank[first][:, 0, :], prod[first])
+        nc.scalar.copy(out=turned[first][:], in_=bank[first][:, 0, :])
+
+        gather(prod[second][:], second, 0, I)
+        page_sums(bank[second][:, 0, :], prod[second])
+        nc.tensor.transpose(bank[second][:, 1, :], turned[first][:], ident[:])
+        nc.scalar.copy(out=turned[second][:], in_=bank[second][:, 0, :])
+        nc.scalar.activation(
+            out=sk[:, :, first : first + 2],
+            in_=bank[second][:, 1, :].unsqueeze(2).to_broadcast([P, G, 2]),
+            func=ACT.Copy,
+            scale=dsc_cols[:, first : first + 1],
+        )
+
+        q_bf = keep.tile([P, Q, PACK], BF16, name="q_bf", tag="chain", align_bytes=64)
         nc.scalar.copy(
             out=q_bf[:].rearrange("p (c i) t -> p c t i", i=4),
             in_=q_raw[:].rearrange("p t (c i) -> p c t i", i=4),
         )
-        q_codes = keep.tile([P, Q], U32, name="q_codes", align_bytes=64)
+
+        gather(prod[third][:], third, 0, I)
+        page_sums(bank[third][:, 0, :], prod[third])
+        nc.tensor.transpose(bank[third][:, 1, :], turned[second][:], ident[:])
+        nc.scalar.copy(out=turned[third][:], in_=bank[third][:, 0, :])
+        nc.tensor.transpose(bank[third][:, 2, :], turned[third][:], ident[:])
+        nc.scalar.copy(out=sk[:, :, second : second + 2], in_=bank[third][:, 1:3, :].rearrange("p t g -> p g t"))
+
+        halves = [
+            keep.tile([P, HALF], F32, name="last_low", tag="late", align_bytes=64),
+            keep.tile([P, HALF], F32, name="last_high"),
+        ]
+        for h in range(2):
+            gather(halves[h][:], last, h * HALF, (h + 1) * HALF)
+        for h in range(2):
+            with nc.allow_low_precision(reason="float32 sum, rounded once for the quantiser"):
+                nc.vector.tensor_reduce(
+                    out=sk[:, h * G // 2 : (h + 1) * G // 2, last],
+                    in_=halves[h][:].rearrange("p (g j) -> p g j", j=PAGE),
+                    axis=AXIS.X,
+                    op=ALU.add,
+                )
+
+        q_codes = keep.tile([P, Q], U32, name="q_codes", tag="late", align_bytes=64)
         q_scales = keep.tile([P, Q], U8, name="q_scales", align_bytes=64)
         nc.vector.quantize_mx(
             out=q_codes[:].bitcast(FP8X4), scales=q_scales[:], in_=q_bf[:].rearrange("p q t -> p (q t)")
@@ -143,10 +150,10 @@ def tile_attend_pagesketch_kernel(tc, query, keys, sg, dsc, bias, offs, offs2, o
             out=sk_codes[:].bitcast(FP8X4), scales=sk_scales[:], in_=sk[:].rearrange("p g t -> p (g t)")
         )
 
-        picked, scores, s, neg_max = [], [], [], []
+        scores, s, neg_max = [], [], []
+        picked = keep.tile([P, 2, G], F32, name="picked", tag="chain", align_bytes=64)
         for h in range(2):
-            picked.append(keep.tile([P, G], F32, name="picked%d" % h))
-            nc.vector.tensor_copy(picked[h][:], bias_rows[:, h * U : (h + 1) * U].indirect(page_list[:]))
+            nc.vector.tensor_copy(picked[:, h, :], bias_rows[:, h * U : (h + 1) * U].indirect(page_list[:]))
             scores.append(once.tile([P, G], F32, name="scores%d" % h))
             rows = slice(h * P, (h + 1) * P)
             nc.tensor.matmul_mx(
@@ -160,7 +167,7 @@ def tile_attend_pagesketch_kernel(tc, query, keys, sg, dsc, bias, offs, offs2, o
             )
         for h in range(2):
             s.append(keep.tile([P, G], F32, name="s%d" % h))
-            nc.vector.tensor_tensor(s[h][:], scores[h][:], picked[h][:], ALU.add)
+            nc.vector.tensor_tensor(s[h][:], scores[h][:], picked[:, h, :], ALU.add)
         for h in range(2):
             neg_max.append(keep.tile([P, 1], F32, name="neg_max%d" % h))
             nc.vector.tensor_reduce(out=neg_max[h][:], in_=s[h][:], axis=AXIS.X, op=ALU.max, negate=True)

@@ -20,7 +20,7 @@ P = 128
 PACK = 4
 PAGE = I // G
 HALF = I // 2
-ORDER = (2, 0, 1, 3)
+ORDER = (0, 1, 2, 3)
 
 
 def tile_attend_pagesketch_kernel(tc, query, keys, sg, dsc, bias, offs, offs2, out):
@@ -33,10 +33,10 @@ def tile_attend_pagesketch_kernel(tc, query, keys, sg, dsc, bias, offs, offs2, o
         slot_list = lists.tile([P, I // 16], U16, name="slot_list")
         page_list = lists.tile([P, G // 16], U16, name="page_list")
 
-        sg_cols = keep.tile([P, 2, 4], F32, name="sg_cols")
+        sg_cols = keep.tile([P, PAGE], F32, name="sg_cols")
         dsc_cols = keep.tile([P, PACK], F32, name="dsc_cols")
         with nc.allow_non_contiguous_dma(reason="short rows of two small vectors"):
-            nc.sync.dma_start(out=sg_cols[:], in_=sg.rearrange("o (h k j) -> k (o h) j", h=2, j=4))
+            nc.sync.dma_start(out=sg_cols[:], in_=sg.rearrange("o (g j) -> g (o j)", j=PAGE))
             nc.scalar.dma_start(out=dsc_cols[:], in_=dsc.rearrange("(p t) o -> p (t o)", t=PACK))
 
         key_rows = keys.rearrange("(p t) n -> t p n", t=PACK)
@@ -62,16 +62,16 @@ def tile_attend_pagesketch_kernel(tc, query, keys, sg, dsc, bias, offs, offs2, o
         for h in range(2):
             spread = once.tile([P, 4, P], F32, name="spread%d" % h)
             for j in range(4):
-                nc.tensor.transpose(spread[:, j, :], sg_cols[:, h, j : j + 1].to_broadcast([P, P]), ident[:])
+                nc.tensor.transpose(spread[:, j, :], sg_cols[:, 4 * h + j : 4 * h + j + 1].to_broadcast([P, P]), ident[:])
             src = spread[:].rearrange("p j k -> p k j")
-            dst = sg_row[:, h * HALF : (h + 1) * HALF].rearrange("p (k j) -> p k j", j=4)
+            dst = sg_row[:].rearrange("p (k j) -> p k j", j=PAGE)[:, :, 4 * h : 4 * h + 4]
             if h == 0:
                 nc.vector.tensor_copy(out=dst, in_=src)
             else:
                 nc.scalar.copy(out=dst, in_=src)
         first, second, third, last = ORDER
-        factor = {first: sg_row}
-        for t in ORDER[1:]:
+        factor = {first: sg_row, second: sg_row}
+        for t in (third, last):
             factor[t] = keep.tile([P, I], F32, name="sg_dsc%d" % t)
             nc.scalar.activation(out=factor[t][:], in_=sg_row[:], func=ACT.Copy, scale=dsc_cols[:, t : t + 1])
 
@@ -88,27 +88,23 @@ def tile_attend_pagesketch_kernel(tc, query, keys, sg, dsc, bias, offs, offs2, o
 
         sk = keep.tile([P, G, PACK], BF16, name="sk", align_bytes=64)
         prod = {t: keep.tile([P, I], F32, name="prod%d" % t) for t in ORDER[:3]}
-        bank = {t: once.tile([P, 3, P], F32, name="bank%d" % t) for t in ORDER[:3]}
-        turned = {
-            first: keep.tile([P, P], F32, name="turned_first", tag="chain", align_bytes=64),
-            second: keep.tile([P, P], F32, name="turned_second"),
-            third: keep.tile([P, P], F32, name="turned_third"),
-        }
+        bank = {t: once.tile([P, 3, P], F32, name="bank%d" % t) for t in ORDER[:2]}
+        turned_first = keep.tile([P, P], F32, name="turned_first", tag="chain", align_bytes=64)
+        turned_second = keep.tile([P, P], F32, name="turned_second")
 
-        gather(prod[first][:, :HALF], first, 0, HALF)
-        gather(prod[first][:, HALF:], first, HALF, I)
+        gather(prod[first][:], first, 0, I)
         page_sums(bank[first][:, 0, :], prod[first])
-        nc.scalar.copy(out=turned[first][:], in_=bank[first][:, 0, :])
-
+        nc.scalar.copy(out=turned_first[:], in_=bank[first][:, 0, :])
         gather(prod[second][:], second, 0, I)
         page_sums(bank[second][:, 0, :], prod[second])
-        nc.tensor.transpose(bank[second][:, 1, :], turned[first][:], ident[:])
-        nc.scalar.copy(out=turned[second][:], in_=bank[second][:, 0, :])
+        nc.tensor.transpose(bank[second][:, 1, :], turned_first[:], ident[:])
+        nc.scalar.copy(out=turned_second[:], in_=bank[second][:, 0, :])
         nc.scalar.activation(
-            out=sk[:, :, first : first + 2],
-            in_=bank[second][:, 1, :].unsqueeze(2).to_broadcast([P, G, 2]),
-            func=ACT.Copy,
-            scale=dsc_cols[:, first : first + 1],
+            out=sk[:, :, first], in_=bank[second][:, 1, :], func=ACT.Copy, scale=dsc_cols[:, first : first + 1]
+        )
+        nc.tensor.transpose(bank[first][:, 1, :], turned_second[:], ident[:])
+        nc.scalar.activation(
+            out=sk[:, :, second], in_=bank[first][:, 1, :], func=ACT.Copy, scale=dsc_cols[:, second : second + 1]
         )
 
         q_bf = keep.tile([P, Q, PACK], BF16, name="q_bf", tag="chain", align_bytes=64)
@@ -118,11 +114,13 @@ def tile_attend_pagesketch_kernel(tc, query, keys, sg, dsc, bias, offs, offs2, o
         )
 
         gather(prod[third][:], third, 0, I)
-        page_sums(bank[third][:, 0, :], prod[third])
-        nc.tensor.transpose(bank[third][:, 1, :], turned[second][:], ident[:])
-        nc.scalar.copy(out=turned[third][:], in_=bank[third][:, 0, :])
-        nc.tensor.transpose(bank[third][:, 2, :], turned[third][:], ident[:])
-        nc.scalar.copy(out=sk[:, :, second : second + 2], in_=bank[third][:, 1:3, :].rearrange("p t g -> p g t"))
+        with nc.allow_low_precision(reason="float32 sum, rounded once for the quantiser"):
+            nc.vector.tensor_reduce(
+                out=sk[:, :, third],
+                in_=prod[third][:].rearrange("p (g j) -> p g j", j=PAGE),
+                axis=AXIS.X,
+                op=ALU.add,
+            )
 
         halves = [
             keep.tile([P, HALF], F32, name="last_low", tag="late", align_bytes=64),

@@ -29,14 +29,15 @@ def tile_attend_pagesketch_kernel(tc, query, keys, sg, dsc, bias, offs, offs2, o
         lists = ctx.enter_context(tc.tile_pool(name="lists", bufs=1))
         keep = ctx.enter_context(tc.tile_pool(name="keep", bufs=1))
         once = ctx.enter_context(tc.psum_pool(name="once", bufs=1))
+        ring = ctx.enter_context(tc.psum_pool(name="ring", bufs=2))
 
         slot_list = lists.tile([P, I // 16], U16, name="slot_list")
         page_list = lists.tile([P, G // 16], U16, name="page_list")
 
         sg_cols = keep.tile([P, PAGE], F32, name="sg_cols")
-        dsc_cols = keep.tile([P, PACK], F32, name="dsc_cols")
+        dsc_cols = keep.tile([P, PACK], F32, name="dsc_cols", tag="scales", align_bytes=64)
         with nc.allow_non_contiguous_dma(reason="short rows of two small vectors"):
-            nc.sync.dma_start(out=sg_cols[:], in_=sg.rearrange("o (g j) -> g (o j)", j=PAGE))
+            nc.scalar.dma_start(out=sg_cols[:], in_=sg.rearrange("o (g j) -> g (o j)", j=PAGE))
             nc.scalar.dma_start(out=dsc_cols[:], in_=dsc.rearrange("(p t) o -> p (t o)", t=PACK))
 
         key_rows = keys.rearrange("(p t) n -> t p n", t=PACK)
@@ -58,54 +59,53 @@ def tile_attend_pagesketch_kernel(tc, query, keys, sg, dsc, bias, offs, offs2, o
         ident = keep.tile([P, P], F32, name="ident")
         make_identity(nc, ident[:])
 
-        sg_row = keep.tile([P, I], F32, name="sg_row")
-        for h in range(2):
-            spread = once.tile([P, 4, P], F32, name="spread%d" % h)
-            for j in range(4):
-                nc.tensor.transpose(spread[:, j, :], sg_cols[:, 4 * h + j : 4 * h + j + 1].to_broadcast([P, P]), ident[:])
-            src = spread[:].rearrange("p j k -> p k j")
-            dst = sg_row[:].rearrange("p (k j) -> p k j", j=PAGE)[:, :, 4 * h : 4 * h + 4]
-            if h == 0:
-                nc.vector.tensor_copy(out=dst, in_=src)
-            else:
-                nc.scalar.copy(out=dst, in_=src)
         first, second, third, last = ORDER
-        factor = {first: sg_row, second: sg_row}
+        factor = {t: keep.tile([P, I], F32, name="sg_dsc%d" % t) for t in (third, last)}
+        spread = []
+        for h in range(2):
+            spread.append(once.tile([P, 4, P], F32, name="spread%d" % h))
+            for j in range(4):
+                column = sg_cols[:, 4 * h + j : 4 * h + j + 1]
+                nc.tensor.transpose(spread[h][:, j, :], column.to_broadcast([P, P]), ident[:])
         for t in (third, last):
-            factor[t] = keep.tile([P, I], F32, name="sg_dsc%d" % t)
-            nc.scalar.activation(out=factor[t][:], in_=sg_row[:], func=ACT.Copy, scale=dsc_cols[:, t : t + 1])
+            for h in range(2):
+                nc.scalar.activation(
+                    out=factor[t][:].rearrange("p (g j) -> p g j", j=PAGE)[:, :, 4 * h : 4 * h + 4],
+                    in_=spread[h][:].rearrange("p j g -> p g j"),
+                    func=ACT.Copy,
+                    scale=dsc_cols[:, t : t + 1],
+                )
 
         def gather(dst, t, lo, hi):
             nc.vector.tensor_tensor(
                 dst, planes[t][:].indirect(slot_list[:, lo // 16 : hi // 16]), factor[t][:, lo:hi], ALU.mult
             )
 
-        def page_sums(dst, prod):
+        sk = keep.tile([P, G, PACK], BF16, name="sk", align_bytes=64)
+        scaled = {}
+        for t in (first, second):
+            tag = "chain" if t == second else "listed_first"
+            listed = keep.tile([P, I], F32, name="listed%d" % t, tag=tag, align_bytes=64)
+            nc.vector.tensor_copy(listed[:], planes[t][:].indirect(slot_list[:]))
+            scaled[t] = keep.tile([P, PAGE, P], F32, name="scaled%d" % t)
+            for h in range(2):
+                turned = ring.tile([P, 4, P], F32, name="turned", tag="bank")
+                for j in range(4):
+                    nc.tensor.transpose(turned[:, j, :], listed[:, 4 * h + j : I : PAGE], ident[:])
+                for j in range(4):
+                    nc.scalar.activation(
+                        out=scaled[t][:, 4 * h + j, :],
+                        in_=turned[:, j, :],
+                        func=ACT.Copy,
+                        scale=sg_cols[:, 4 * h + j : 4 * h + j + 1],
+                    )
+        for t in (first, second):
+            summed = ring.tile([P, G], F32, name="summed", tag="bank")
             for j in range(PAGE):
                 nc.tensor.matmul(
-                    dst, prod[:, j:I:PAGE], ident[:], start=(j == 0), stop=(j == PAGE - 1), is_transpose=True
+                    summed[:], scaled[t][:, j, :], ident[:], start=(j == 0), stop=(j == PAGE - 1), is_transpose=True
                 )
-
-        sk = keep.tile([P, G, PACK], BF16, name="sk", align_bytes=64)
-        prod = {t: keep.tile([P, I], F32, name="prod%d" % t) for t in ORDER[:3]}
-        bank = {t: once.tile([P, 3, P], F32, name="bank%d" % t) for t in ORDER[:2]}
-        turned_first = keep.tile([P, P], F32, name="turned_first", tag="chain", align_bytes=64)
-        turned_second = keep.tile([P, P], F32, name="turned_second")
-
-        gather(prod[first][:], first, 0, I)
-        page_sums(bank[first][:, 0, :], prod[first])
-        nc.scalar.copy(out=turned_first[:], in_=bank[first][:, 0, :])
-        gather(prod[second][:], second, 0, I)
-        page_sums(bank[second][:, 0, :], prod[second])
-        nc.tensor.transpose(bank[second][:, 1, :], turned_first[:], ident[:])
-        nc.scalar.copy(out=turned_second[:], in_=bank[second][:, 0, :])
-        nc.scalar.activation(
-            out=sk[:, :, first], in_=bank[second][:, 1, :], func=ACT.Copy, scale=dsc_cols[:, first : first + 1]
-        )
-        nc.tensor.transpose(bank[first][:, 1, :], turned_second[:], ident[:])
-        nc.scalar.activation(
-            out=sk[:, :, second], in_=bank[first][:, 1, :], func=ACT.Copy, scale=dsc_cols[:, second : second + 1]
-        )
+            nc.scalar.activation(out=sk[:, :, t], in_=summed[:], func=ACT.Copy, scale=dsc_cols[:, t : t + 1])
 
         q_bf = keep.tile([P, Q, PACK], BF16, name="q_bf", tag="chain", align_bytes=64)
         nc.scalar.copy(
@@ -113,32 +113,24 @@ def tile_attend_pagesketch_kernel(tc, query, keys, sg, dsc, bias, offs, offs2, o
             in_=q_raw[:].rearrange("p t (c i) -> p c t i", i=4),
         )
 
-        gather(prod[third][:], third, 0, I)
-        with nc.allow_low_precision(reason="float32 sum, rounded once for the quantiser"):
-            nc.vector.tensor_reduce(
-                out=sk[:, :, third],
-                in_=prod[third][:].rearrange("p (g j) -> p g j", j=PAGE),
-                axis=AXIS.X,
-                op=ALU.add,
-            )
-
-        halves = [
-            keep.tile([P, HALF], F32, name="last_low", tag="late", align_bytes=64),
-            keep.tile([P, HALF], F32, name="last_high"),
-        ]
-        for h in range(2):
-            gather(halves[h][:], last, h * HALF, (h + 1) * HALF)
-        for h in range(2):
-            with nc.allow_low_precision(reason="float32 sum, rounded once for the quantiser"):
-                nc.vector.tensor_reduce(
-                    out=sk[:, h * G // 2 : (h + 1) * G // 2, last],
-                    in_=halves[h][:].rearrange("p (g j) -> p g j", j=PAGE),
-                    axis=AXIS.X,
-                    op=ALU.add,
-                )
+        for t in (third, last):
+            halves = [
+                keep.tile([P, HALF], F32, name="low%d" % t, tag="late" if t == last else "early", align_bytes=64),
+                keep.tile([P, HALF], F32, name="high%d" % t),
+            ]
+            for h in range(2):
+                gather(halves[h][:], t, h * HALF, (h + 1) * HALF)
+            for h in range(2):
+                with nc.allow_low_precision(reason="float32 sum, rounded once for the quantiser"):
+                    nc.vector.tensor_reduce(
+                        out=sk[:, h * G // 2 : (h + 1) * G // 2, t],
+                        in_=halves[h][:].rearrange("p (g j) -> p g j", j=PAGE),
+                        axis=AXIS.X,
+                        op=ALU.add,
+                    )
 
         q_codes = keep.tile([P, Q], U32, name="q_codes", tag="late", align_bytes=64)
-        q_scales = keep.tile([P, Q], U8, name="q_scales", align_bytes=64)
+        q_scales = keep.tile([P, Q], U8, name="q_scales", tag="scales", align_bytes=64)
         nc.vector.quantize_mx(
             out=q_codes[:].bitcast(FP8X4), scales=q_scales[:], in_=q_bf[:].rearrange("p q t -> p (q t)")
         )

from contextlib import ExitStack

import concourse.mybir as mybir
from concourse.masks import make_identity

D, T, I, G, U, Q = 512, 2048, 1024, 128, 512, 256
FLOPS = 2 * D * Q * G

F32 = mybir.dt.float32
BF16 = mybir.dt.bfloat16
U32 = mybir.dt.uint32
U16 = mybir.dt.uint16
U8 = mybir.dt.uint8
FP8X4 = mybir.dt.float8_e4m3fn_x4
ALU = mybir.AluOpType
ACT = mybir.ActivationFunctionType
AXIS = mybir.AxisListType

P = 128
PACK = 4
PAGE = I // G
HALF = I // 2
ORDER = (0, 1, 2, 3)


def tile_attend_pagesketch_kernel(tc, query, keys, sg, dsc, bias, offs, offs2, out):
    nc = tc.nc
    with ExitStack() as ctx:
        lists = ctx.enter_context(tc.tile_pool(name="lists", bufs=1))
        keep = ctx.enter_context(tc.tile_pool(name="keep", bufs=1))
        once = ctx.enter_context(tc.psum_pool(name="once", bufs=1))
        ring = ctx.enter_context(tc.psum_pool(name="ring", bufs=2))

        slot_list = lists.tile([P, I // 16], U16, name="slot_list")
        page_list = lists.tile([P, G // 16], U16, name="page_list")

        sg_cols = keep.tile([P, PAGE], F32, name="sg_cols")
        dsc_cols = keep.tile([P, PACK], F32, name="dsc_cols", tag="scales", align_bytes=64)
        with nc.allow_non_contiguous_dma(reason="short rows of two small vectors"):
            nc.scalar.dma_start(out=sg_cols[:], in_=sg.rearrange("o (g j) -> g (o j)", j=PAGE))
            nc.scalar.dma_start(out=dsc_cols[:], in_=dsc.rearrange("(p t) o -> p (t o)", t=PACK))

        key_rows = keys.rearrange("(p t) n -> t p n", t=PACK)
        planes = {}
        for n, t in enumerate(ORDER):
            planes[t] = keep.tile([P, T], F32, name="keys%d" % t)
            nc.sync.dma_start(out=planes[t][:], in_=key_rows[t])
            if n == 0:
                nc.sync.dma_start(slot_list[:], offs)
        q_raw = keep.tile([P, PACK, Q], F32, name="q_raw")
        nc.sync.dma_start(out=q_raw[:], in_=query.rearrange("(p t) q -> p t q", t=PACK))
        nc.sync.dma_start(page_list[:], offs2)
        bias_rows = keep.tile([P, 2 * U], F32, name="bias_rows")
        nc.sync.dma_start(
            out=bias_rows[:].rearrange("p (h u) -> p h u", h=2),
            in_=bias.rearrange("(h p) u -> p h u", h=2),
        )

        ident = keep.tile([P, P], F32, name="ident")
        make_identity(nc, ident[:])

        first, second, third, last = ORDER
        factor = {t: keep.tile([P, I], F32, name="sg_dsc%d" % t) for t in (third, last)}
        spread = []
        for h in range(2):
            spread.append(once.tile([P, 4, P], F32, name="spread%d" % h))
            for j in range(4):
                column = sg_cols[:, 4 * h + j : 4 * h + j + 1]
                nc.tensor.transpose(spread[h][:, j, :], column.to_broadcast([P, P]), ident[:])
        for t in (third, last):
            for h in range(2):
                nc.scalar.activation(
                    out=factor[t][:].rearrange("p (g j) -> p g j", j=PAGE)[:, :, 4 * h : 4 * h + 4],
                    in_=spread[h][:].rearrange("p j g -> p g j"),
                    func=ACT.Copy,
                    scale=dsc_cols[:, t : t + 1],
                )

        def gather(dst, t, lo, hi):
            nc.vector.tensor_tensor(
                dst, planes[t][:].indirect(slot_list[:, lo // 16 : hi // 16]), factor[t][:, lo:hi], ALU.mult
            )

        sk = keep.tile([P, G, PACK], BF16, name="sk", align_bytes=64)
        scaled = {}
        for t in (first, second):
            tag = "chain" if t == second else "listed_first"
            listed = keep.tile([P, I], F32, name="listed%d" % t, tag=tag, align_bytes=64)
            nc.vector.tensor_copy(listed[:], planes[t][:].indirect(slot_list[:]))
            scaled[t] = keep.tile([P, PAGE, P], F32, name="scaled%d" % t)
            for h in range(2):
                turned = ring.tile([P, 4, P], F32, name="turned", tag="bank")
                for j in range(4):
                    nc.tensor.transpose(turned[:, j, :], listed[:, 4 * h + j : I : PAGE], ident[:])
                for j in range(4):
                    nc.scalar.activation(
                        out=scaled[t][:, 4 * h + j, :],
                        in_=turned[:, j, :],
                        func=ACT.Copy,
                        scale=sg_cols[:, 4 * h + j : 4 * h + j + 1],
                    )
        for t in (first, second):
            summed = ring.tile([P, G], F32, name="summed", tag="bank")
            for j in range(PAGE):
                nc.tensor.matmul(
                    summed[:], scaled[t][:, j, :], ident[:], start=(j == 0), stop=(j == PAGE - 1), is_transpose=True
                )
            nc.scalar.activation(out=sk[:, :, t], in_=summed[:], func=ACT.Copy, scale=dsc_cols[:, t : t + 1])

        q_bf = keep.tile([P, Q, PACK], BF16, name="q_bf", tag="chain", align_bytes=64)
        nc.scalar.copy(
            out=q_bf[:].rearrange("p (c i) t -> p c t i", i=4),
            in_=q_raw[:].rearrange("p t (c i) -> p c t i", i=4),
        )

        for t in (third, last):
            halves = [
                keep.tile([P, HALF], F32, name="low%d" % t, tag="late" if t == last else "early", align_bytes=64),
                keep.tile([P, HALF], F32, name="high%d" % t),
            ]
            for h in range(2):
                gather(halves[h][:], t, h * HALF, (h + 1) * HALF)
            for h in range(2):
                with nc.allow_low_precision(reason="float32 sum, rounded once for the quantiser"):
                    nc.vector.tensor_reduce(
                        out=sk[:, h * G // 2 : (h + 1) * G // 2, t],
                        in_=halves[h][:].rearrange("p (g j) -> p g j", j=PAGE),
                        axis=AXIS.X,
                        op=ALU.add,
                    )

        q_codes = keep.tile([P, Q], U32, name="q_codes", tag="late", align_bytes=64)
        q_scales = keep.tile([P, Q], U8, name="q_scales", tag="scales", align_bytes=64)
        nc.vector.quantize_mx(
            out=q_codes[:].bitcast(FP8X4), scales=q_scales[:], in_=q_bf[:].rearrange("p q t -> p (q t)")
        )
        sk_codes = keep.tile([P, G], U32, name="sk_codes", align_bytes=64)
        sk_scales = keep.tile([P, G], U8, name="sk_scales", align_bytes=64)
        nc.vector.quantize_mx(
            out=sk_codes[:].bitcast(FP8X4), scales=sk_scales[:], in_=sk[:].rearrange("p g t -> p (g t)")
        )

        scores, s, neg_max = [], [], []
        picked = keep.tile([P, 2, G], F32, name="picked", tag="chain", align_bytes=64)
        for h in range(2):
            nc.vector.tensor_copy(picked[:, h, :], bias_rows[:, h * U : (h + 1) * U].indirect(page_list[:]))
            scores.append(once.tile([P, G], F32, name="scores%d" % h))
            rows = slice(h * P, (h + 1) * P)
            nc.tensor.matmul_mx(
                out=scores[h][:],
                lhsT=q_codes[:, rows].bitcast(FP8X4),
                lhsT_scale=q_scales[:, rows],
                rhs=sk_codes[:].bitcast(FP8X4),
                rhs_scale=sk_scales[:],
                start=True,
                stop=True,
            )
        for h in range(2):
            s.append(keep.tile([P, G], F32, name="s%d" % h))
            nc.vector.tensor_tensor(s[h][:], scores[h][:], picked[:, h, :], ALU.add)
        for h in range(2):
            neg_max.append(keep.tile([P, 1], F32, name="neg_max%d" % h))
            nc.vector.tensor_reduce(out=neg_max[h][:], in_=s[h][:], axis=AXIS.X, op=ALU.max, negate=True)
        for h in range(2):
            p = keep.tile([P, G], F32, name="p%d" % h)
            total = keep.tile([P, 1], F32, name="total%d" % h)
            nc.scalar.activation(out=p[:], in_=s[h][:], func=ACT.Exp, bias=neg_max[h][:], accum_out=total[:])
            inverse = keep.tile([P, 1], F32, name="inverse%d" % h)
            nc.vector.reciprocal(inverse[:], total[:])
            y = keep.tile([P, G], F32, name="y%d" % h)
            nc.vector.tensor_scalar(y[:], p[:], inverse[:], float(G), ALU.mult, ALU.mult)
            nc.sync.dma_start(out=out[h * P : (h + 1) * P, :], in_=y[:])
